import numpy as np
import ml_dtypes


def mxq(x, axis, fmt="e4m3"):
    dtype, down = {"e4m3": (ml_dtypes.float8_e4m3fn, 7), "e5m2": (ml_dtypes.float8_e5m2, 14)}[fmt]
    v = np.moveaxis(np.asarray(x, np.float32).astype(ml_dtypes.bfloat16).astype(np.float64), axis, -1)
    blocks = v.reshape(v.shape[:-1] + (-1, 32))
    amax = np.abs(blocks).max(-1, keepdims=True)
    byte = np.maximum(np.where(amax > 0, np.frexp(amax)[1] - 1 + 127, 0) - down, 1)
    scale = np.exp2(byte - 127.0)
    codes = (blocks / scale).astype(np.float32).astype(dtype).astype(np.float64)
    return np.moveaxis((codes * scale).reshape(v.shape), -1, axis)


WIDE = False


def mx_kscale(k):
    if not WIDE:
        return np.ones(k)
    levels = np.array([10, -10, 5, -5, 0])
    if k % 512:
        return np.exp2(np.random.permutation(np.resize(levels, k // 32))).repeat(32)
    a = np.empty((k // 512, 16))
    for p in range(k // 512):
        a[p, :8] = np.random.permutation(np.resize(levels, 8))
        for g in range(8):
            far = levels[np.abs(levels - a[p, g]) >= 10]
            a[p, g + 8] = far[np.random.randint(len(far))]
    return np.exp2(a.ravel()).repeat(32)


def f64(x):
    return np.asarray(x).astype(np.float64)


def striped(idx):
    return np.tile(np.asarray(idx).reshape(-1, 16).T, (8, 1)).astype(np.uint16)


def unstriped(offs):
    return offs[:16].T.reshape(-1).astype(np.int64)


E2M1 = np.array([0.0, 0.5, 1.0, 1.5, 2.0, 3.0, 4.0, 6.0, -0.0, -0.5, -1.0, -1.5, -2.0, -3.0, -4.0, -6.0])


def pack_weight(w, fmt):
    k, n = w.shape
    w = f64(np.asarray(w, np.float32).astype(ml_dtypes.bfloat16)).reshape(k // 32, 32, n)
    amax = np.abs(w).max(1)
    if fmt == "e4m3":
        byte = np.frexp(amax)[1] - 1 + 127 - 7
    else:
        mant, ex = np.frexp(amax / 6.0)
        byte = np.where(mant > 0.5, ex, ex - 1) + 127
    byte = np.clip(np.where(amax > 0, byte, 1), 1, 254)
    scaled = (w * np.exp2(127.0 - byte)[:, None, :]).reshape(k, n).astype(np.float32)
    by_word = np.ascontiguousarray(scaled.reshape(k // 512, 128, 4, n).transpose(0, 1, 3, 2))
    if fmt == "e4m3":
        words = by_word.astype(ml_dtypes.float8_e4m3fn).view(np.uint8)
    else:
        c = by_word.astype(ml_dtypes.float4_e2m1fn).view(np.uint8) & 0xF
        words = (c[..., 0::2] | (c[..., 1::2] << 4)).reshape(k // 512, 128, 2 * n)
    return np.ascontiguousarray(words), np.ascontiguousarray(byte.astype(np.uint8).reshape(k // 512, 16, n))


def unpack_weight(words, scales, fmt):
    g, _, n = scales.shape
    words = np.ascontiguousarray(words).reshape(g, 128, n, -1)
    if fmt == "e4m3":
        vals = words.view(ml_dtypes.float8_e4m3fn).astype(np.float64)
    else:
        nib = np.empty((g, 128, n, 4), np.uint8)
        nib[..., 0::2] = words & 0xF
        nib[..., 1::2] = words >> 4
        vals = E2M1[nib]
    vals = vals * np.repeat(np.exp2(scales.astype(np.float64) - 127.0), 8, axis=1)[..., None]
    return vals.transpose(0, 1, 3, 2).reshape(g * 512, n)


def bf(x):
    return np.asarray(x, np.float32).astype(ml_dtypes.bfloat16)


def planes(Y):
    r, m = Y.shape
    b = f64(bf(Y)).reshape(r // 32, 32, m)
    amax = np.abs(b).max(1)
    byte = np.clip(np.where(amax > 0, np.frexp(amax)[1] - 1 + 127 - 7, 1), 1, 254)
    codes = (b * np.exp2(127.0 - byte)[:, None, :]).reshape(r, m).astype(np.float32).astype(ml_dtypes.float8_e4m3fn).view(np.uint8)
    words = codes.reshape(r // 512, 128, 4, m).transpose(0, 1, 3, 2)
    return np.ascontiguousarray(words), np.ascontiguousarray(byte.astype(np.uint8).reshape(r // 512, 16, m))


K, T, J, N = 1024, 2048, 512, 512


def setup_inputs():
    n = np.random.standard_normal
    idx = np.random.permutation(T)[:J]
    fk = mx_kscale(K)
    wap = pack_weight(n((K, N)) * 1 / np.sqrt(K) * fk[:, None], "e2m1")
    wbp = pack_weight(n((K, N)) * np.random.uniform(0.2, 1.6, (K, 1)) / np.sqrt(K) * fk[:, None], "e4m3")
    wcp = pack_weight(n((K, N)) * 0.6 / np.sqrt(K) * fk[:, None], "e2m1")
    return {
        "xt": (n((K, T)) * np.random.uniform(0.3, 1.7, (1, T)) / fk[:, None]).astype(np.float32),
        "wa_words": wap[0],
        "wa_scales": wap[1],
        "wb_words": wbp[0],
        "wb_scales": wbp[1],
        "wc_words": wcp[0],
        "wc_scales": wcp[1],
        "bi": (np.random.uniform(-0.5, 0.5, (1, N))).astype(np.float32),
        "offs": striped(idx),
    }


def reference(xt, wa_words, wa_scales, wb_words, wb_scales, wc_words, wc_scales, bi, offs):
    idx = unstriped(offs)
    wau = unpack_weight(wa_words, wa_scales, "e2m1")
    wbu = unpack_weight(wb_words, wb_scales, "e4m3")
    wcu = unpack_weight(wc_words, wc_scales, "e2m1")
    xtidxq = mxq(f64(xt)[:, idx], 0, "e4m3")
    a = xtidxq.T @ wau
    b = xtidxq.T @ wbu
    e = xtidxq.T @ wcu
    ea = np.exp(np.mean(np.square(a), axis=1, keepdims=True))
    eb = np.exp(np.mean(np.square(b), axis=1, keepdims=True))
    ec = np.exp(np.mean(np.square(e), axis=1, keepdims=True))
    y = (ea * a + eb * b + ec * e) / (ea + eb + ec) + f64(bi)
    words, scales = planes(y)
    return y, words, scales

@@ -1,0 +1,171 @@
+from contextlib import ExitStack
+import math
+
+import concourse.mybir as mybir
+from concourse.masks import make_identity
+
+K, T, J, N = 1024, 2048, 512, 512
+FLOPS = 3 * 2 * K * J * N
+
+F32 = mybir.dt.float32
+BF16 = mybir.dt.bfloat16
+I32 = mybir.dt.int32
+U32 = mybir.dt.uint32
+U16 = mybir.dt.uint16
+U8 = mybir.dt.uint8
+FP8X4 = mybir.dt.float8_e4m3fn_x4
+FP4X4 = mybir.dt.float4_e2m1fn_x4
+ALU = mybir.AluOpType
+ACT = mybir.ActivationFunctionType
+AXIS = mybir.AxisListType
+
+P = 128
+PACK = 4
+PASSES = K // (P * PACK)
+EXPERTS = 3
+BANKS = 8
+HALF = N // 2
+CAST_SPLIT = 352
+
+
+def tile_moe_three_experts_by_energy_pl_kernel(
+    tc, xt, wa_words, wa_scales, wb_words, wb_scales, wc_words, wc_scales, bi, offs, out_0, out_1, out_2
+):
+    nc = tc.nc
+    with ExitStack() as ctx:
+        keep = ctx.enter_context(tc.tile_pool(name="keep", bufs=1))
+        ring = ctx.enter_context(tc.tile_pool(name="ring", bufs=2))
+        psum = ctx.enter_context(tc.psum_pool(name="psum", bufs=1))
+
+        offsets = keep.tile([P, J // 16], U16, name="offsets")
+        bias_cols = keep.tile([P, PACK], F32, name="bias_cols")
+        nc.gpsimd.dma_start(bias_cols[:], bi.rearrange("o (p c) -> (o p) c", c=PACK))
+
+        w_scales = []
+        for e, scale_input in enumerate([wa_scales, wb_scales, wc_scales]):
+            plane = keep.tile([P, PASSES, N], U8, name="plane%d" % e, align_bytes=64)
+            nc.vector.memset(plane[:].bitcast(I32), 0)
+            for q in range(4):
+                nc.scalar.dma_start(
+                    plane[32 * q : 32 * q + 4].bitcast(I32),
+                    scale_input[:, 4 * q : 4 * q + 4, :].rearrange("g q n -> q g n").bitcast(I32),
+                )
+            w_scales.append(plane)
+
+        word_inputs = [wa_words, wb_words.rearrange("g p n r -> g p (n r)"), wc_words]
+        word_dtypes = [FP4X4, FP8X4, FP4X4]
+        w_words = {}
+
+        def load_words(e, passes):
+            width = word_inputs[e].shape[2]
+            words = keep.tile([P, len(passes), width], U8, name="words%d%d" % (e, passes[0]), align_bytes=64)
+            source = word_inputs[e][passes[0] : passes[-1] + 1].rearrange("g p n -> p g n")
+            nc.sync.dma_start(words[:].bitcast(I32), source.bitcast(I32))
+            for slot, g in enumerate(passes):
+                w_words[g, e] = words[:, slot, :]
+
+        x_rows = xt.rearrange("(g p r) t -> g r p t", g=PASSES, r=PACK)
+        windows = {}
+        for g in range(PASSES):
+            for r in range(PACK):
+                if (g, r) == (PASSES - 1, PACK - 1):
+                    load_words(0, (0,))
+                windows[g, r] = keep.tile([P, T], F32, name="window%d%d" % (g, r))
+                nc.sync.dma_start(windows[g, r][:], x_rows[g, r])
+                if (g, r) == (0, 0):
+                    nc.sync.dma_start(offsets[:], offs)
+        for e, passes in [(1, (0,)), (2, (0, 1)), (0, (1,)), (1, (1,))]:
+            load_words(e, passes)
+
+        identity = keep.tile([P, P], F32, name="identity")
+        make_identity(nc, identity[:])
+        spread = psum.tile([P, PACK, P], F32, name="spread", tag="bank%d" % (BANKS - 1))
+        for c in range(PACK):
+            nc.tensor.transpose(spread[:, c, :], bias_cols[:, c : c + 1].to_broadcast([P, P]), identity[:])
+        bias = keep.tile([P, N], F32, name="bias")
+        nc.scalar.activation(
+            bias[:].rearrange("i (p c) -> i p c", c=PACK), spread[:].rearrange("i c p -> i p c"), ACT.Copy
+        )
+
+        x_codes, x_scales = [], []
+        for g in range(PASSES):
+            grouped = keep.tile([P, J * PACK], BF16, name="grouped%d" % g, align_bytes=64)
+            dealt = grouped[:].rearrange("p (t m r) -> p m t r", t=PACK, r=PACK)
+            for r in range(PACK):
+                nc.vector.tensor_copy(dealt[:, :, :, r], windows[g, r][:].indirect(offsets[:]))
+            codes = keep.tile([P, J], U32, name="x_codes%d" % g, align_bytes=64)
+            scales = keep.tile([P, J], U8, name="x_scales%d" % g, align_bytes=64)
+            pieces = 1 if g < PASSES - 1 else PACK
+            width = J // pieces
+            for s in range(pieces):
+                cols = slice(s * width, (s + 1) * width)
+                nc.vector.quantize_mx(
+                    out=codes[:, cols].bitcast(FP8X4),
+                    scales=scales[:, cols],
+                    in_=grouped[:, s * width * PACK : (s + 1) * width * PACK],
+                )
+            x_codes.append(codes)
+            x_scales.append(scales)
+
+        y = keep.tile([P, PACK, N], F32, name="y")
+        y_rows = out_0.rearrange("(p t) n -> p t n", t=PACK)
+        for t in range(PACK):
+            cols = slice(t * P, (t + 1) * P)
+            sums = []
+            for e in range(EXPERTS):
+                sums.append(psum.tile([P, N], F32, name="sums%d%d" % (t, e), tag="bank%d" % ((EXPERTS * t + e) % BANKS)))
+            for g in range(PASSES):
+                for e in range(EXPERTS):
+                    nc.tensor.matmul_mx(
+                        out=sums[e][:],
+                        lhsT=x_codes[g][:, cols].bitcast(FP8X4),
+                        lhsT_scale=x_scales[g][:, cols],
+                        rhs=w_words[g, e].bitcast(word_dtypes[e]),
+                        rhs_scale=w_scales[e][:, g, :],
+                        start=(g == 0),
+                        stop=(g == PASSES - 1),
+                    )
+            energy = keep.tile([P, EXPERTS], F32, name="energy%d" % t)
+            for e in range(EXPERTS):
+                squares = ring.tile([P, N], F32, name="squares")
+                nc.scalar.activation(
+                    squares[:], sums[e][:], ACT.Square, scale=1.0 / math.sqrt(N), accum_out=energy[:, e : e + 1]
+                )
+            minus_max = keep.tile([P, 1], F32, name="minus_max%d" % t)
+            nc.vector.tensor_reduce(minus_max[:], energy[:], AXIS.X, ALU.max, negate=True)
+            exps = keep.tile([P, EXPERTS], F32, name="exps%d" % t)
+            total = keep.tile([P, 1], F32, name="total%d" % t)
+            nc.scalar.activation(exps[:], energy[:], ACT.Exp, bias=minus_max[:], accum_out=total[:])
+            inverse = keep.tile([P, 1], F32, name="inverse%d" % t)
+            nc.vector.reciprocal(inverse[:], total[:])
+            shares = keep.tile([P, EXPERTS], F32, name="shares%d" % t)
+            nc.vector.tensor_scalar(shares[:], exps[:], inverse[:], None, ALU.mult)
+            partial = [bias[:, 0:HALF], bias[:, HALF:N]]
+            for e in range(EXPERTS):
+                for h in range(2):
+                    half = slice(h * HALF, (h + 1) * HALF)
+                    if e < EXPERTS - 1:
+                        target = ring.tile([P, HALF], F32, name="partial%d%d" % (e, h))[:]
+                    else:
+                        target = y[:, t, half]
+                    nc.vector.scalar_tensor_tensor(
+                        target, sums[e][:, half], shares[:, e : e + 1], partial[h], ALU.mult, ALU.add
+                    )
+                    partial[h] = target
+            nc.sync.dma_start(y_rows[:, t, :], y[:, t, :])
+
+        y_grouped = keep.tile([P, N, PACK], BF16, name="y_grouped", align_bytes=64)
+        y_dealt = y[:].rearrange("p t n -> p n t")
+        nc.vector.tensor_copy(y_grouped[:, :CAST_SPLIT, :], y_dealt[:, :CAST_SPLIT, :])
+        nc.scalar.copy(y_grouped[:, CAST_SPLIT:, :], y_dealt[:, CAST_SPLIT:, :])
+        y_codes = keep.tile([P, N], U32, name="y_codes", align_bytes=64)
+        y_scales = keep.tile([P, N], U8, name="y_scales", align_bytes=64)
+        nc.vector.quantize_mx(
+            out=y_codes[:].bitcast(FP8X4), scales=y_scales[:], in_=y_grouped[:].rearrange("p n t -> p (n t)")
+        )
+        nc.sync.dma_start(out_1[0].rearrange("p n r -> p (n r)").bitcast(I32), y_codes[:].bitcast(I32))
+        for q in range(4):
+            queue = nc.scalar if q % 2 == 0 else nc.sync
+            queue.dma_start(
+                out_2[0, 4 * q : 4 * q + 4, :].bitcast(I32), y_scales[32 * q : 32 * q + 4, :].bitcast(I32)
+            )

@@ -26,6 +26,11 @@ EXPERTS = 3
 BANKS = 8
 HALF = N // 2
 CAST_SPLIT = 352
+RUN = 4
+
+
+def interleave(copy, grouped, planar):
+    copy(grouped.rearrange("p (c i) r -> p c r i", i=RUN), planar.rearrange("p r (c i) -> p c r i", i=RUN))
 
 
 def tile_moe_three_experts_by_energy_pl_kernel(
@@ -41,16 +46,27 @@ def tile_moe_three_experts_by_energy_pl_kernel(
         bias_cols = keep.tile([P, PACK], F32, name="bias_cols")
         nc.gpsimd.dma_start(bias_cols[:], bi.rearrange("o (p c) -> (o p) c", c=PACK))
 
-        w_scales = []
-        for e, scale_input in enumerate([wa_scales, wb_scales, wc_scales]):
-            plane = keep.tile([P, PASSES, N], U8, name="plane%d" % e, align_bytes=64)
-            nc.vector.memset(plane[:].bitcast(I32), 0)
-            for q in range(4):
-                nc.scalar.dma_start(
-                    plane[32 * q : 32 * q + 4].bitcast(I32),
-                    scale_input[:, 4 * q : 4 * q + 4, :].rearrange("g q n -> q g n").bitcast(I32),
-                )
-            w_scales.append(plane)
+        scale_inputs = [wa_scales, wb_scales, wc_scales]
+        planes, w_scales = {}, {}
+        for e in (0, 2):
+            planes[e] = keep.tile([P, PASSES, N], U8, name="plane%d" % e, align_bytes=64)
+            nc.vector.memset(planes[e][:].bitcast(I32), 0)
+            for g in range(PASSES):
+                w_scales[g, e] = planes[e][:, g, :]
+        packed = keep.tile([P, N], U8, name="packed", align_bytes=64)
+        nc.vector.memset(packed[:].bitcast(I32), 0)
+        for g in range(PASSES):
+            w_scales[g, 1] = packed[4 * (g + 1) :, :]
+        for q in range(4):
+            nc.gpsimd.dma_start(
+                packed[32 * q + 4 : 32 * q + 12, :].bitcast(I32), wb_scales[:, 4 * q : 4 * q + 4, :].bitcast(I32)
+            )
+
+        def load_scales(queue, e, q):
+            queue.dma_start(
+                planes[e][32 * q : 32 * q + 4].bitcast(I32),
+                scale_inputs[e][:, 4 * q : 4 * q + 4, :].rearrange("g q n -> q g n").bitcast(I32),
+            )
 
         word_inputs = [wa_words, wb_words.rearrange("g p n r -> g p (n r)"), wc_words]
         word_dtypes = [FP4X4, FP8X4, FP4X4]
@@ -64,17 +80,30 @@ def tile_moe_three_experts_by_energy_pl_kernel(
             for slot, g in enumerate(passes):
                 w_words[g, e] = words[:, slot, :]
 
-        x_rows = xt.rearrange("(g p r) t -> g r p t", g=PASSES, r=PACK)
+        x_rows = xt.rearrange("(g p r) t -> g p r t", g=PASSES, r=PACK)
         windows = {}
-        for g in range(PASSES):
-            for r in range(PACK):
-                if (g, r) == (PASSES - 1, PACK - 1):
-                    load_words(0, (0,))
-                windows[g, r] = keep.tile([P, T], F32, name="window%d%d" % (g, r))
-                nc.sync.dma_start(windows[g, r][:], x_rows[g, r])
-                if (g, r) == (0, 0):
-                    nc.sync.dma_start(offsets[:], offs)
-        for e, passes in [(1, (0,)), (2, (0, 1)), (0, (1,)), (1, (1,))]:
+
+        def load_rows(g, first, count):
+            rows = keep.tile([P, count, T], F32, name="rows%d%d" % (g, first))
+            nc.sync.dma_start(rows[:], x_rows[g, :, first : first + count, :])
+            for slot in range(count):
+                windows[g, first + slot] = rows[:, slot, :]
+
+        small_loads = [(e, q) for e in (0, 2) for q in range(4)]
+        load_rows(0, 0, 2)
+        nc.sync.dma_start(offsets[:], offs)
+        load_rows(0, 2, 2)
+        for e, q in small_loads[:5]:
+            load_scales(nc.sync, e, q)
+        load_rows(1, 0, 2)
+        load_scales(nc.sync, *small_loads[5])
+        load_rows(1, 2, 1)
+        for e, q in small_loads[6:]:
+            load_scales(nc.sync, e, q)
+        load_words(0, (0,))
+        load_words(2, (0,))
+        load_rows(1, 3, 1)
+        for e, passes in [(1, (0,)), (0, (1,)), (2, (1,)), (1, (1,))]:
             load_words(e, passes)
 
         identity = keep.tile([P, P], F32, name="identity")
@@ -87,30 +116,43 @@ def tile_moe_three_experts_by_energy_pl_kernel(
             bias[:].rearrange("i (p c) -> i p c", c=PACK), spread[:].rearrange("i c p -> i p c"), ACT.Copy
         )
 
-        x_codes, x_scales = [], []
+        grouped = {}
         for g in range(PASSES):
-            grouped = keep.tile([P, J * PACK], BF16, name="grouped%d" % g, align_bytes=64)
-            dealt = grouped[:].rearrange("p (t m r) -> p m t r", t=PACK, r=PACK)
+            planar = keep.tile([P, PACK, J], BF16, name="planar%d" % g)
             for r in range(PACK):
-                nc.vector.tensor_copy(dealt[:, :, :, r], windows[g, r][:].indirect(offsets[:]))
-            codes = keep.tile([P, J], U32, name="x_codes%d" % g, align_bytes=64)
-            scales = keep.tile([P, J], U8, name="x_scales%d" % g, align_bytes=64)
+                dealt = planar[:, r, :].rearrange("p (t m) -> p m t", t=PACK)
+                nc.vector.tensor_copy(dealt, windows[g, r].indirect(offsets[:]))
             pieces = 1 if g < PASSES - 1 else PACK
             width = J // pieces
+            grouped[g] = []
             for s in range(pieces):
-                cols = slice(s * width, (s + 1) * width)
+                grouped[g].append(keep.tile([P, width, PACK], BF16, name="grouped%d%d" % (g, s), align_bytes=64))
+                copy = nc.vector.tensor_copy if s % 2 == 0 else nc.scalar.copy
+                interleave(copy, grouped[g][s][:], planar[:, :, s * width : (s + 1) * width])
+            if g == 0:
+                first_codes = keep.tile([P, J], U32, name="first_codes", align_bytes=64)
+                first_scales = keep.tile([P, J], U8, name="first_scales", align_bytes=64)
                 nc.vector.quantize_mx(
-                    out=codes[:, cols].bitcast(FP8X4),
-                    scales=scales[:, cols],
-                    in_=grouped[:, s * width * PACK : (s + 1) * width * PACK],
+                    out=first_codes[:].bitcast(FP8X4), scales=first_scales[:], in_=grouped[0][0][:].rearrange("p c r -> p (c r)")
                 )
-            x_codes.append(codes)
-            x_scales.append(scales)
 
         y = keep.tile([P, PACK, N], F32, name="y")
         y_rows = out_0.rearrange("(p t) n -> p t n", t=PACK)
         for t in range(PACK):
             cols = slice(t * P, (t + 1) * P)
+            last_codes = keep.tile(
+                [P, P], U32, name="last_codes%d" % t, tag="last_codes%d" % (0 if t == 1 else t), align_bytes=64
+            )
+            last_scales = keep.tile(
+                [P, P], U8, name="last_scales%d" % t, tag="last_scales%d" % (0 if t == 2 else t), align_bytes=64
+            )
+            nc.vector.quantize_mx(
+                out=last_codes[:].bitcast(FP8X4),
+                scales=last_scales[:],
+                in_=grouped[1][t][:].rearrange("p c r -> p (c r)"),
+            )
+            x_codes = [first_codes[:, cols], last_codes[:]]
+            x_scales = [first_scales[:, cols], last_scales[:]]
             sums = []
             for e in range(EXPERTS):
                 sums.append(psum.tile([P, N], F32, name="sums%d%d" % (t, e), tag="bank%d" % ((EXPERTS * t + e) % BANKS)))
@@ -118,19 +160,28 @@ def tile_moe_three_experts_by_energy_pl_kernel(
                 for e in range(EXPERTS):
                     nc.tensor.matmul_mx(
                         out=sums[e][:],
-                        lhsT=x_codes[g][:, cols].bitcast(FP8X4),
-                        lhsT_scale=x_scales[g][:, cols],
+                        lhsT=x_codes[g].bitcast(FP8X4),
+                        lhsT_scale=x_scales[g],
                         rhs=w_words[g, e].bitcast(word_dtypes[e]),
-                        rhs_scale=w_scales[e][:, g, :],
+                        rhs_scale=w_scales[g, e],
                         start=(g == 0),
                         stop=(g == PASSES - 1),
                     )
             energy = keep.tile([P, EXPERTS], F32, name="energy%d" % t)
             for e in range(EXPERTS):
-                squares = ring.tile([P, N], F32, name="squares")
-                nc.scalar.activation(
-                    squares[:], sums[e][:], ACT.Square, scale=1.0 / math.sqrt(N), accum_out=energy[:, e : e + 1]
-                )
+                if (t, e) == (0, 0):
+                    stats = keep.tile([P, 6], F32, name="stats%d" % t)
+                    nc.vector.bn_stats(stats[:], sums[e][:])
+                    moments = keep.tile([P, 2], F32, name="moments%d" % t)
+                    nc.vector.bn_aggr(moments[:], stats[:])
+                    nc.vector.scalar_tensor_tensor(
+                        energy[:, e : e + 1], moments[:, 0:1], moments[:, 0:1], moments[:, 1:2], ALU.mult, ALU.add
+                    )
+                else:
+                    squares = ring.tile([P, N], F32, name="squares")
+                    nc.scalar.activation(
+                        squares[:], sums[e][:], ACT.Square, scale=1.0 / math.sqrt(N), accum_out=energy[:, e : e + 1]
+                    )
             minus_max = keep.tile([P, 1], F32, name="minus_max%d" % t)
             nc.vector.tensor_reduce(minus_max[:], energy[:], AXIS.X, ALU.max, negate=True)
             exps = keep.tile([P, EXPERTS], F32, name="exps%d" % t)
@@ -154,16 +205,19 @@ def tile_moe_three_experts_by_energy_pl_kernel(
                     partial[h] = target
             nc.sync.dma_start(y_rows[:, t, :], y[:, t, :])
 
-        y_grouped = keep.tile([P, N, PACK], BF16, name="y_grouped", align_bytes=64)
-        y_dealt = y[:].rearrange("p t n -> p n t")
-        nc.vector.tensor_copy(y_grouped[:, :CAST_SPLIT, :], y_dealt[:, :CAST_SPLIT, :])
-        nc.scalar.copy(y_grouped[:, CAST_SPLIT:, :], y_dealt[:, CAST_SPLIT:, :])
-        y_codes = keep.tile([P, N], U32, name="y_codes", align_bytes=64)
+        y_grouped = [keep.tile([P, HALF, PACK], BF16, name="y_grouped%d" % h, align_bytes=64) for h in range(2)]
+        interleave(nc.vector.tensor_copy, y_grouped[0][:], y[:, :, :HALF])
+        interleave(nc.vector.tensor_copy, y_grouped[1][:, : CAST_SPLIT - HALF, :], y[:, :, HALF:CAST_SPLIT])
+        interleave(nc.scalar.copy, y_grouped[1][:, CAST_SPLIT - HALF :, :], y[:, :, CAST_SPLIT:])
         y_scales = keep.tile([P, N], U8, name="y_scales", align_bytes=64)
-        nc.vector.quantize_mx(
-            out=y_codes[:].bitcast(FP8X4), scales=y_scales[:], in_=y_grouped[:].rearrange("p n t -> p (n t)")
-        )
-        nc.sync.dma_start(out_1[0].rearrange("p n r -> p (n r)").bitcast(I32), y_codes[:].bitcast(I32))
+        word_rows = out_1[0].rearrange("p n r -> p (n r)").bitcast(I32)
+        for h in range(2):
+            half = slice(h * HALF, (h + 1) * HALF)
+            y_codes = keep.tile([P, HALF], U32, name="y_codes%d" % h, align_bytes=64)
+            nc.vector.quantize_mx(
+                out=y_codes[:].bitcast(FP8X4), scales=y_scales[:, half], in_=y_grouped[h][:].rearrange("p n t -> p (n t)")
+            )
+            nc.sync.dma_start(word_rows[:, half], y_codes[:].bitcast(I32))
         for q in range(4):
             queue = nc.scalar if q % 2 == 0 else nc.sync
             queue.dma_start(

from contextlib import ExitStack
import math

import concourse.mybir as mybir
from concourse.masks import make_identity

K, T, J, N = 1024, 2048, 512, 512
FLOPS = 3 * 2 * K * J * N

F32 = mybir.dt.float32
BF16 = mybir.dt.bfloat16
I32 = mybir.dt.int32
U32 = mybir.dt.uint32
U16 = mybir.dt.uint16
U8 = mybir.dt.uint8
FP8X4 = mybir.dt.float8_e4m3fn_x4
FP4X4 = mybir.dt.float4_e2m1fn_x4
ALU = mybir.AluOpType
ACT = mybir.ActivationFunctionType
AXIS = mybir.AxisListType

P = 128
PACK = 4
PASSES = K // (P * PACK)
EXPERTS = 3
BANKS = 8
HALF = N // 2
CAST_SPLIT = 352
RUN = 4


def interleave(copy, grouped, planar):
    copy(grouped.rearrange("p (c i) r -> p c r i", i=RUN), planar.rearrange("p r (c i) -> p c r i", i=RUN))


def tile_moe_three_experts_by_energy_pl_kernel(
    tc, xt, wa_words, wa_scales, wb_words, wb_scales, wc_words, wc_scales, bi, offs, out_0, out_1, out_2
):
    nc = tc.nc
    with ExitStack() as ctx:
        keep = ctx.enter_context(tc.tile_pool(name="keep", bufs=1))
        ring = ctx.enter_context(tc.tile_pool(name="ring", bufs=2))
        psum = ctx.enter_context(tc.psum_pool(name="psum", bufs=1))

        offsets = keep.tile([P, J // 16], U16, name="offsets")
        bias_cols = keep.tile([P, PACK], F32, name="bias_cols")
        nc.gpsimd.dma_start(bias_cols[:], bi.rearrange("o (p c) -> (o p) c", c=PACK))

        scale_inputs = [wa_scales, wb_scales, wc_scales]
        planes, w_scales = {}, {}
        for e in (0, 2):
            planes[e] = keep.tile([P, PASSES, N], U8, name="plane%d" % e, align_bytes=64)
            nc.vector.memset(planes[e][:].bitcast(I32), 0)
            for g in range(PASSES):
                w_scales[g, e] = planes[e][:, g, :]
        packed = keep.tile([P, N], U8, name="packed", align_bytes=64)
        nc.vector.memset(packed[:].bitcast(I32), 0)
        for g in range(PASSES):
            w_scales[g, 1] = packed[4 * (g + 1) :, :]
        for q in range(4):
            nc.gpsimd.dma_start(
                packed[32 * q + 4 : 32 * q + 12, :].bitcast(I32), wb_scales[:, 4 * q : 4 * q + 4, :].bitcast(I32)
            )

        def load_scales(queue, e, q):
            queue.dma_start(
                planes[e][32 * q : 32 * q + 4].bitcast(I32),
                scale_inputs[e][:, 4 * q : 4 * q + 4, :].rearrange("g q n -> q g n").bitcast(I32),
            )

        word_inputs = [wa_words, wb_words.rearrange("g p n r -> g p (n r)"), wc_words]
        word_dtypes = [FP4X4, FP8X4, FP4X4]
        w_words = {}

        def load_words(e, passes):
            width = word_inputs[e].shape[2]
            words = keep.tile([P, len(passes), width], U8, name="words%d%d" % (e, passes[0]), align_bytes=64)
            source = word_inputs[e][passes[0] : passes[-1] + 1].rearrange("g p n -> p g n")
            nc.sync.dma_start(words[:].bitcast(I32), source.bitcast(I32))
            for slot, g in enumerate(passes):
                w_words[g, e] = words[:, slot, :]

        x_rows = xt.rearrange("(g p r) t -> g p r t", g=PASSES, r=PACK)
        windows = {}

        def load_rows(g, first, count):
            rows = keep.tile([P, count, T], F32, name="rows%d%d" % (g, first))
            nc.sync.dma_start(rows[:], x_rows[g, :, first : first + count, :])
            for slot in range(count):
                windows[g, first + slot] = rows[:, slot, :]

        small_loads = [(e, q) for e in (0, 2) for q in range(4)]
        load_rows(0, 0, 2)
        nc.sync.dma_start(offsets[:], offs)
        load_rows(0, 2, 2)
        for e, q in small_loads[:5]:
            load_scales(nc.sync, e, q)
        load_rows(1, 0, 2)
        load_scales(nc.sync, *small_loads[5])
        load_rows(1, 2, 1)
        for e, q in small_loads[6:]:
            load_scales(nc.sync, e, q)
        load_words(0, (0,))
        load_words(2, (0,))
        load_rows(1, 3, 1)
        for e, passes in [(1, (0,)), (0, (1,)), (2, (1,)), (1, (1,))]:
            load_words(e, passes)

        identity = keep.tile([P, P], F32, name="identity")
        make_identity(nc, identity[:])
        spread = psum.tile([P, PACK, P], F32, name="spread", tag="bank%d" % (BANKS - 1))
        for c in range(PACK):
            nc.tensor.transpose(spread[:, c, :], bias_cols[:, c : c + 1].to_broadcast([P, P]), identity[:])
        bias = keep.tile([P, N], F32, name="bias")
        nc.scalar.activation(
            bias[:].rearrange("i (p c) -> i p c", c=PACK), spread[:].rearrange("i c p -> i p c"), ACT.Copy
        )

        grouped = {}
        for g in range(PASSES):
            planar = keep.tile([P, PACK, J], BF16, name="planar%d" % g)
            for r in range(PACK):
                dealt = planar[:, r, :].rearrange("p (t m) -> p m t", t=PACK)
                nc.vector.tensor_copy(dealt, windows[g, r].indirect(offsets[:]))
            pieces = 1 if g < PASSES - 1 else PACK
            width = J // pieces
            grouped[g] = []
            for s in range(pieces):
                grouped[g].append(keep.tile([P, width, PACK], BF16, name="grouped%d%d" % (g, s), align_bytes=64))
                copy = nc.vector.tensor_copy if s % 2 == 0 else nc.scalar.copy
                interleave(copy, grouped[g][s][:], planar[:, :, s * width : (s + 1) * width])
            if g == 0:
                first_codes = keep.tile([P, J], U32, name="first_codes", align_bytes=64)
                first_scales = keep.tile([P, J], U8, name="first_scales", align_bytes=64)
                nc.vector.quantize_mx(
                    out=first_codes[:].bitcast(FP8X4), scales=first_scales[:], in_=grouped[0][0][:].rearrange("p c r -> p (c r)")
                )

        y = keep.tile([P, PACK, N], F32, name="y")
        y_rows = out_0.rearrange("(p t) n -> p t n", t=PACK)
        for t in range(PACK):
            cols = slice(t * P, (t + 1) * P)
            last_codes = keep.tile(
                [P, P], U32, name="last_codes%d" % t, tag="last_codes%d" % (0 if t == 1 else t), align_bytes=64
            )
            last_scales = keep.tile(
                [P, P], U8, name="last_scales%d" % t, tag="last_scales%d" % (0 if t == 2 else t), align_bytes=64
            )
            nc.vector.quantize_mx(
                out=last_codes[:].bitcast(FP8X4),
                scales=last_scales[:],
                in_=grouped[1][t][:].rearrange("p c r -> p (c r)"),
            )
            x_codes = [first_codes[:, cols], last_codes[:]]
            x_scales = [first_scales[:, cols], last_scales[:]]
            sums = []
            for e in range(EXPERTS):
                sums.append(psum.tile([P, N], F32, name="sums%d%d" % (t, e), tag="bank%d" % ((EXPERTS * t + e) % BANKS)))
            for g in range(PASSES):
                for e in range(EXPERTS):
                    nc.tensor.matmul_mx(
                        out=sums[e][:],
                        lhsT=x_codes[g].bitcast(FP8X4),
                        lhsT_scale=x_scales[g],
                        rhs=w_words[g, e].bitcast(word_dtypes[e]),
                        rhs_scale=w_scales[g, e],
                        start=(g == 0),
                        stop=(g == PASSES - 1),
                    )
            energy = keep.tile([P, EXPERTS], F32, name="energy%d" % t)
            for e in range(EXPERTS):
                if (t, e) == (0, 0):
                    stats = keep.tile([P, 6], F32, name="stats%d" % t)
                    nc.vector.bn_stats(stats[:], sums[e][:])
                    moments = keep.tile([P, 2], F32, name="moments%d" % t)
                    nc.vector.bn_aggr(moments[:], stats[:])
                    nc.vector.scalar_tensor_tensor(
                        energy[:, e : e + 1], moments[:, 0:1], moments[:, 0:1], moments[:, 1:2], ALU.mult, ALU.add
                    )
                else:
                    squares = ring.tile([P, N], F32, name="squares")
                    nc.scalar.activation(
                        squares[:], sums[e][:], ACT.Square, scale=1.0 / math.sqrt(N), accum_out=energy[:, e : e + 1]
                    )
            minus_max = keep.tile([P, 1], F32, name="minus_max%d" % t)
            nc.vector.tensor_reduce(minus_max[:], energy[:], AXIS.X, ALU.max, negate=True)
            exps = keep.tile([P, EXPERTS], F32, name="exps%d" % t)
            total = keep.tile([P, 1], F32, name="total%d" % t)
            nc.scalar.activation(exps[:], energy[:], ACT.Exp, bias=minus_max[:], accum_out=total[:])
            inverse = keep.tile([P, 1], F32, name="inverse%d" % t)
            nc.vector.reciprocal(inverse[:], total[:])
            shares = keep.tile([P, EXPERTS], F32, name="shares%d" % t)
            nc.vector.tensor_scalar(shares[:], exps[:], inverse[:], None, ALU.mult)
            partial = [bias[:, 0:HALF], bias[:, HALF:N]]
            for e in range(EXPERTS):
                for h in range(2):
                    half = slice(h * HALF, (h + 1) * HALF)
                    if e < EXPERTS - 1:
                        target = ring.tile([P, HALF], F32, name="partial%d%d" % (e, h))[:]
                    else:
                        target = y[:, t, half]
                    nc.vector.scalar_tensor_tensor(
                        target, sums[e][:, half], shares[:, e : e + 1], partial[h], ALU.mult, ALU.add
                    )
                    partial[h] = target
            nc.sync.dma_start(y_rows[:, t, :], y[:, t, :])

        y_grouped = [keep.tile([P, HALF, PACK], BF16, name="y_grouped%d" % h, align_bytes=64) for h in range(2)]
        interleave(nc.vector.tensor_copy, y_grouped[0][:], y[:, :, :HALF])
        interleave(nc.vector.tensor_copy, y_grouped[1][:, : CAST_SPLIT - HALF, :], y[:, :, HALF:CAST_SPLIT])
        interleave(nc.scalar.copy, y_grouped[1][:, CAST_SPLIT - HALF :, :], y[:, :, CAST_SPLIT:])
        y_scales = keep.tile([P, N], U8, name="y_scales", align_bytes=64)
        word_rows = out_1[0].rearrange("p n r -> p (n r)").bitcast(I32)
        for h in range(2):
            half = slice(h * HALF, (h + 1) * HALF)
            y_codes = keep.tile([P, HALF], U32, name="y_codes%d" % h, align_bytes=64)
            nc.vector.quantize_mx(
                out=y_codes[:].bitcast(FP8X4), scales=y_scales[:, half], in_=y_grouped[h][:].rearrange("p n t -> p (n t)")
            )
            nc.sync.dma_start(word_rows[:, half], y_codes[:].bitcast(I32))
        for q in range(4):
            queue = nc.scalar if q % 2 == 0 else nc.sync
            queue.dma_start(
                out_2[0, 4 * q : 4 * q + 4, :].bitcast(I32), y_scales[32 * q : 32 * q + 4, :].bitcast(I32)
            )
